import numpy as np
import ml_dtypes


def mxq(x, axis, fmt="e4m3"):
    dtype, down = {"e4m3": (ml_dtypes.float8_e4m3fn, 7), "e5m2": (ml_dtypes.float8_e5m2, 14)}[fmt]
    v = np.moveaxis(np.asarray(x, np.float32).astype(ml_dtypes.bfloat16).astype(np.float64), axis, -1)
    blocks = v.reshape(v.shape[:-1] + (-1, 32))
    amax = np.abs(blocks).max(-1, keepdims=True)
    byte = np.maximum(np.where(amax > 0, np.frexp(amax)[1] - 1 + 127, 0) - down, 1)
    scale = np.exp2(byte - 127.0)
    codes = (blocks / scale).astype(np.float32).astype(dtype).astype(np.float64)
    return np.moveaxis((codes * scale).reshape(v.shape), -1, axis)


WIDE = False


def mx_kscale(k):
    if not WIDE:
        return np.ones(k)
    levels = np.array([10, -10, 5, -5, 0])
    if k % 512:
        return np.exp2(np.random.permutation(np.resize(levels, k // 32))).repeat(32)
    a = np.empty((k // 512, 16))
    for p in range(k // 512):
        a[p, :8] = np.random.permutation(np.resize(levels, 8))
        for g in range(8):
            far = levels[np.abs(levels - a[p, g]) >= 10]
            a[p, g + 8] = far[np.random.randint(len(far))]
    return np.exp2(a.ravel()).repeat(32)


def f64(x):
    return np.asarray(x).astype(np.float64)


def striped(idx):
    return np.tile(np.asarray(idx).reshape(-1, 16).T, (8, 1)).astype(np.uint16)


def unstriped(offs):
    return offs[:16].T.reshape(-1).astype(np.int64)


E2M1 = np.array([0.0, 0.5, 1.0, 1.5, 2.0, 3.0, 4.0, 6.0, -0.0, -0.5, -1.0, -1.5, -2.0, -3.0, -4.0, -6.0])


def pack_weight(w, fmt):
    k, n = w.shape
    w = f64(np.asarray(w, np.float32).astype(ml_dtypes.bfloat16)).reshape(k // 32, 32, n)
    amax = np.abs(w).max(1)
    if fmt == "e4m3":
        byte = np.frexp(amax)[1] - 1 + 127 - 7
    else:
        mant, ex = np.frexp(amax / 6.0)
        byte = np.where(mant > 0.5, ex, ex - 1) + 127
    byte = np.clip(np.where(amax > 0, byte, 1), 1, 254)
    scaled = (w * np.exp2(127.0 - byte)[:, None, :]).reshape(k, n).astype(np.float32)
    by_word = np.ascontiguousarray(scaled.reshape(k // 512, 128, 4, n).transpose(0, 1, 3, 2))
    if fmt == "e4m3":
        words = by_word.astype(ml_dtypes.float8_e4m3fn).view(np.uint8)
    else:
        c = by_word.astype(ml_dtypes.float4_e2m1fn).view(np.uint8) & 0xF
        words = (c[..., 0::2] | (c[..., 1::2] << 4)).reshape(k // 512, 128, 2 * n)
    return np.ascontiguousarray(words), np.ascontiguousarray(byte.astype(np.uint8).reshape(k // 512, 16, n))


def unpack_weight(words, scales, fmt):
    g, _, n = scales.shape
    words = np.ascontiguousarray(words).reshape(g, 128, n, -1)
    if fmt == "e4m3":
        vals = words.view(ml_dtypes.float8_e4m3fn).astype(np.float64)
    else:
        nib = np.empty((g, 128, n, 4), np.uint8)
        nib[..., 0::2] = words & 0xF
        nib[..., 1::2] = words >> 4
        vals = E2M1[nib]
    vals = vals * np.repeat(np.exp2(scales.astype(np.float64) - 127.0), 8, axis=1)[..., None]
    return vals.transpose(0, 1, 3, 2).reshape(g * 512, n)


def softplus(v):
    return np.log(1.0 + np.exp(v))


def sigmoid(v):
    return 1.0 / (1.0 + np.exp(-v))


K, R, F, T, J, M = 512, 128, 512, 2048, 512, 256


def setup_inputs():
    n = np.random.standard_normal
    idx = np.random.permutation(T)[:J]
    idx2 = np.random.permutation(J)[:M]
    idx3 = np.random.permutation(J)[:M]
    fk = mx_kscale(K)
    ff = mx_kscale(F)
    tabp = pack_weight(n((K, T)) / fk[:, None], "e2m1")
    return {
        "tab_words": tabp[0],
        "tab_scales": tabp[1],
        "w1": (n((K, R)) * 1 / np.sqrt(K) * fk[:, None]).astype(np.float32),
        "bias": (np.random.uniform(-0.5, 0.5, (R, 1))).astype(np.float32),
        "reserve": (np.random.uniform(0.3, 1.0, (R, 1))).astype(np.float32),
        "wo": (n((F, R)) * 1 / np.sqrt(F) * ff[:, None]).astype(np.float32),
        "dy": (n((F, M)) / ff[:, None]).astype(np.float32),
        "og": (np.random.uniform(0.3, 1.0, (R, 1))).astype(np.float32),
        "base": (0.3 * n((R, J))).astype(np.float32),
        "offs": striped(idx),
        "offs2": striped(idx2),
        "offs3": striped(idx3),
    }


def reference(tab_words, tab_scales, w1, bias, reserve, wo, dy, og, base, offs, offs2, offs3):
    idx = unstriped(offs)
    idx2 = unstriped(offs2)
    idx3 = unstriped(offs3)
    tabu = unpack_weight(tab_words, tab_scales, "e2m1")
    w1q = mxq(f64(w1), 0, "e4m3")
    tabidxg = tabu[:, idx]
    a = w1q.T @ tabidxg
    h1 = softplus(a + f64(bias))
    s = h1[:, idx2] * h1[:, idx3]
    woq = mxq(f64(wo), 0, "e4m3")
    dyq = mxq(f64(dy), 0, "e4m3")
    c0 = woq.T @ dyq
    ds = c0 / (s + h1[:, idx2] + f64(reserve)) - c0 * s / np.square(s + h1[:, idx2] + f64(reserve))
    e1 = c0 * s / np.square(s + h1[:, idx2] + f64(reserve)) * (-1.0)
    s1 = np.zeros((R, J))
    s1[:, idx2] = e1
    e2 = ds * h1[:, idx3]
    s2 = np.zeros((R, J))
    s2[:, idx2] = e2
    e3 = ds * h1[:, idx2]
    s3 = np.zeros((R, J))
    s3[:, idx3] = e3
    dh1 = s1 + s2 + s3
    da = dh1 * sigmoid(a + f64(bias))
    hda = da * 2.0
    hdh1 = hda * sigmoid(a + f64(bias))
    he3 = hdh1[:, idx3]
    he2 = hdh1[:, idx2]
    he1 = hdh1[:, idx2]
    hds = he3 * h1[:, idx2] + he2 * h1[:, idx3]
    hs = he1 * (-1.0) / np.square(s + h1[:, idx2] + f64(reserve)) * c0 + he1 * (-1.0) * c0 * s / np.square(np.square(s + h1[:, idx2] + f64(reserve))) * (-1.0) * (s + h1[:, idx2] + f64(reserve)) * 2.0 + hds * (-1.0) / np.square(s + h1[:, idx2] + f64(reserve)) * c0 + hds * (-1.0) * c0 * s / np.square(np.square(s + h1[:, idx2] + f64(reserve))) * (-1.0) * (s + h1[:, idx2] + f64(reserve)) * 2.0 - hds * c0 / np.square(s + h1[:, idx2] + f64(reserve))
    e51 = he3 * ds
    s51 = np.zeros((R, J))
    s51[:, idx2] = e51
    e52 = he1 * (-1.0) * c0 * s / np.square(np.square(s + h1[:, idx2] + f64(reserve))) * (-1.0) * (s + h1[:, idx2] + f64(reserve)) * 2.0
    s52 = np.zeros((R, J))
    s52[:, idx2] = e52
    e53 = hds * c0 / np.square(s + h1[:, idx2] + f64(reserve)) * (-1.0)
    s53 = np.zeros((R, J))
    s53[:, idx2] = e53
    e54 = hds * (-1.0) * c0 * s / np.square(np.square(s + h1[:, idx2] + f64(reserve))) * (-1.0) * (s + h1[:, idx2] + f64(reserve)) * 2.0
    s54 = np.zeros((R, J))
    s54[:, idx2] = e54
    e55 = hs * h1[:, idx3]
    s55 = np.zeros((R, J))
    s55[:, idx2] = e55
    e56 = he2 * ds
    s56 = np.zeros((R, J))
    s56[:, idx3] = e56
    e57 = hs * h1[:, idx2]
    s57 = np.zeros((R, J))
    s57[:, idx3] = e57
    hh1 = s51 + s52 + s53 + s54 + s55 + s56 + s57
    ha = hda * dh1 * sigmoid(a + f64(bias)) * (1.0 - sigmoid(a + f64(bias))) + hh1 * sigmoid(a + f64(bias))
    y = ha * f64(og) + f64(base)
    return y

@@ -1,0 +1,211 @@
+import math
+from contextlib import ExitStack
+
+import concourse.mybir as mybir
+
+K, R, F, T, J, M = 512, 128, 512, 2048, 512, 256
+FLOPS = 2 * K * R * J + 2 * F * R * M
+
+F32 = mybir.dt.float32
+BF16 = mybir.dt.bfloat16
+I32 = mybir.dt.int32
+U32 = mybir.dt.uint32
+U16 = mybir.dt.uint16
+U8 = mybir.dt.uint8
+FP8X4 = mybir.dt.float8_e4m3fn_x4
+FP4X4 = mybir.dt.float4_e2m1fn_x4
+ACT = mybir.ActivationFunctionType
+ALU = mybir.AluOpType
+
+P = 128
+PACK = 4
+HALF = J // 2
+LIST_ROWS = 16
+TINY = 2.0 ** -60
+
+
+def tile_attend_gppairshare_kernel(tc, tab_words, tab_scales, w1, bias, reserve, wo, dy, og, base, offs, offs2, offs3, out):
+    nc = tc.nc
+    halves = [slice(h * HALF, (h + 1) * HALF) for h in range(2)]
+
+    with ExitStack() as ctx:
+        lists = ctx.enter_context(tc.tile_pool(name="lists", bufs=1))
+        sb = ctx.enter_context(tc.tile_pool(name="sb", bufs=1))
+        ps = ctx.enter_context(tc.psum_pool(name="ps", bufs=1))
+
+        def f32(name, width):
+            return sb.tile([P, width], F32, name=name, align_bytes=64)
+
+        table_scales = sb.tile([P, T], U8, name="table_scales", align_bytes=64)
+        nc.gpsimd.memset(table_scales[:].bitcast(I32), 0)
+        first2, first3, second2, second3 = (f32(n, J) for n in ("first2", "first3", "second2", "second3"))
+        for window in (first2, first3, second2, second3):
+            nc.vector.memset(window[:], 0.0)
+
+        slots = lists.tile([P, J // LIST_ROWS], U16, name="slots")
+        nc.sync.dma_start(slots[:], offs)
+        w1_raw = sb.tile([P, PACK, R], F32, name="w1_raw")
+        nc.sync.dma_start(w1_raw[:], w1.rearrange("(p t) n -> p t n", t=PACK))
+        table_words = sb.tile([P, T], U16, name="table_words", align_bytes=64)
+        nc.sync.dma_start(table_words[:].bitcast(I32), tab_words[0].bitcast(I32))
+        for quad in range(4):
+            nc.scalar.dma_start(
+                table_scales[32 * quad : 32 * quad + 4, :].bitcast(I32),
+                tab_scales[0, 4 * quad : 4 * quad + 4, :].bitcast(I32),
+            )
+        bias_col = f32("bias_col", 1)
+        nc.sync.dma_start(bias_col[:], bias)
+        dy_raw = sb.tile([P, PACK, M], F32, name="dy_raw")
+        nc.sync.dma_start(dy_raw[:], dy.rearrange("(p t) n -> p t n", t=PACK))
+        wo_raw = sb.tile([P, PACK, R], F32, name="wo_raw")
+        nc.sync.dma_start(wo_raw[:], wo.rearrange("(p t) n -> p t n", t=PACK))
+        list2 = lists.tile([P, M // LIST_ROWS], U16, name="list2")
+        nc.sync.dma_start(list2[:], offs2)
+        list3 = lists.tile([P, M // LIST_ROWS], U16, name="list3")
+        nc.sync.dma_start(list3[:], offs3)
+        rho = f32("rho", 1)
+        nc.sync.dma_start(rho[:], reserve)
+        gain = f32("gain", 1)
+        nc.sync.dma_start(gain[:], og)
+        base_sb = f32("base_sb", J)
+        nc.sync.dma_start(base_sb[:], base)
+
+        neg_bias = f32("neg_bias", 1)
+        nc.gpsimd.tensor_scalar(neg_bias[:], bias_col[:], -1.0, 0.0, ALU.mult, ALU.add)
+
+        def interleave(copy, raw, width, name):
+            grouped = sb.tile([P, width, PACK], BF16, name=name + "_bf16", align_bytes=64)
+            copy(grouped[:], raw[:].rearrange("p t n -> p n t"))
+            return grouped
+
+        def quantize(grouped, width, name):
+            codes = sb.tile([P, width], U32, name=name + "_codes", align_bytes=64)
+            scales = sb.tile([P, width], U8, name=name + "_scales", align_bytes=64)
+            nc.vector.quantize_mx(codes[:].bitcast(FP8X4), scales[:], grouped[:].rearrange("p n t -> p (n t)"))
+            return codes, scales
+
+        w1_codes, w1_scales = quantize(interleave(nc.vector.tensor_copy, w1_raw, R, "w1"), R, "w1")
+        picked_scales = sb.tile([P, J], U8, name="picked_scales", align_bytes=64)
+        nc.vector.tensor_copy(picked_scales[:], table_scales[:].indirect(slots[:]))
+
+        picked = []
+        for h in range(2):
+            cols = slice(h * HALF // LIST_ROWS, (h + 1) * HALF // LIST_ROWS)
+            words = sb.tile([P, HALF], U16, name="picked_words%d" % h, align_bytes=64)
+            nc.vector.tensor_copy(words[:], table_words[:].indirect(slots[:, cols]))
+            picked.append(words)
+
+        z = f32("z", J)
+        nsig = f32("nsig", J)
+        log_nsig = f32("log_nsig", J)
+        h1 = f32("h1", J)
+        sums = []
+        for h in range(2):
+            a = ps.tile([P, HALF], F32, name="a%d" % h)
+            nc.tensor.matmul_mx(
+                a[:], w1_codes[:].bitcast(FP8X4), w1_scales[:],
+                picked[h][:].bitcast(FP4X4), picked_scales[:, halves[h]], start=True, stop=True,
+            )
+            nc.scalar.activation(nsig[:, halves[h]], a[:], ACT.Sigmoid, bias=neg_bias[:], scale=-1.0)
+            sums.append(a)
+        for h in range(2):
+            nc.vector.tensor_scalar(z[:, halves[h]], sums[h][:], bias_col[:], None, ALU.add)
+
+        dy_codes, dy_scales = quantize(interleave(nc.vector.tensor_copy, dy_raw, M, "dy"), M, "dy")
+        wo_codes, wo_scales = quantize(interleave(nc.vector.tensor_copy, wo_raw, R, "wo"), R, "wo")
+        c0 = ps.tile([P, M], F32, name="c0")
+        nc.tensor.matmul_mx(
+            c0[:], wo_codes[:].bitcast(FP8X4), wo_scales[:], dy_codes[:].bitcast(FP8X4), dy_scales[:],
+            start=True, stop=True,
+        )
+
+        for h in range(2):
+            nc.scalar.activation(log_nsig[:, halves[h]], nsig[:, halves[h]], ACT.Ln, bias=TINY)
+        for h in range(2):
+            nc.vector.scalar_tensor_tensor(
+                h1[:, halves[h]], log_nsig[:, halves[h]], -1.0, z[:, halves[h]], ALU.mult, ALU.max
+            )
+
+        u = f32("u", M)
+        v = f32("v", M)
+        nc.vector.tensor_copy(u[:], h1[:].indirect(list2[:]))
+        nc.vector.tensor_copy(v[:], h1[:].indirect(list3[:]))
+        t = f32("t", M)
+        nc.vector.scalar_tensor_tensor(t[:], v[:], 1.0, u[:], ALU.add, ALU.mult)
+        root = f32("root", M)
+        nc.scalar.activation(root[:], t[:], ACT.Abs_reciprocal_sqrt, bias=rho[:])
+        sig = f32("sig", J)
+        r_abs = sig[:, 0:M]
+        nc.scalar.activation(r_abs, root[:], ACT.Square)
+        r2 = f32("r2", M)
+        nc.scalar.activation(r2[:], r_abs, ACT.Square)
+
+        vr = f32("vr", M)
+        nc.vector.tensor_scalar(vr[:], v[:], rho[:], None, ALU.mult)
+        uw = f32("uw", M)
+        nc.vector.scalar_tensor_tensor(uw[:], u[:], rho[:], u[:], ALU.add, ALU.mult)
+        y1 = f32("y1", M)
+        nc.vector.scalar_tensor_tensor(y1[:], v[:], 1.0, u[:], ALU.subtract, ALU.mult)
+        a1 = f32("a1", M)
+        nc.vector.scalar_tensor_tensor(a1[:], v[:], 1.0, vr[:], ALU.add, ALU.mult)
+        c1 = f32("c1", M)
+        nc.vector.tensor_tensor(c1[:], uw[:], u[:], ALU.mult)
+        b1 = f32("b1", M)
+        nc.vector.tensor_scalar(b1[:], y1[:], rho[:], rho[:], ALU.subtract, ALU.mult)
+
+        k2 = f32("k2", M)
+        nc.vector.tensor_tensor(k2[:], r2[:], c0[:], ALU.mult)
+        r_signed = f32("r_signed", M)
+        nc.vector.scalar_tensor_tensor(r_signed[:], t[:], rho[:], r2[:], ALU.add, ALU.mult)
+        nc.vector.tensor_tensor(first2[:].indirect(list2[:]), vr[:], k2[:], ALU.mult)
+        nc.vector.tensor_tensor(first3[:].indirect(list3[:]), uw[:], k2[:], ALU.mult)
+
+        nc.scalar.activation(sig[:], nsig[:], ACT.Identity, bias=1.0, scale=-1.0)
+        sig2 = f32("sig2", J)
+        nc.scalar.activation(sig2[:], sig[:], ACT.Square)
+        gq = f32("gq", J)
+        nc.scalar.activation(gq[:], sig[:], ACT.Square, bias=-0.5)
+
+        dh1 = f32("dh1", J)
+        hdh1 = f32("hdh1", J)
+        for h in range(2):
+            nc.vector.tensor_tensor(dh1[:, halves[h]], first2[:, halves[h]], first3[:, halves[h]], ALU.add)
+        for h in range(2):
+            nc.vector.scalar_tensor_tensor(
+                hdh1[:, halves[h]], dh1[:, halves[h]], 2.0, sig2[:, halves[h]], ALU.mult, ALU.mult
+            )
+        k3 = f32("k3", M)
+        nc.vector.scalar_tensor_tensor(k3[:], r_signed[:], -1.0, k2[:], ALU.mult, ALU.mult)
+        sq = f32("sq", J)
+        nc.scalar.activation(sq[:], dh1[:], ACT.Square, scale=math.sqrt(2.0))
+
+        p = f32("p", M)
+        q = f32("q", M)
+        nc.vector.tensor_copy(p[:], hdh1[:].indirect(list2[:]))
+        nc.vector.tensor_copy(q[:], hdh1[:].indirect(list3[:]))
+        pa, qb, pb, qc, e2, e3 = (f32(n, M) for n in ("pa", "qb", "pb", "qc", "e2", "e3"))
+        nc.vector.tensor_tensor(pa[:], p[:], a1[:], ALU.mult)
+        nc.vector.tensor_tensor(pb[:], p[:], b1[:], ALU.mult)
+        nc.vector.tensor_tensor(qb[:], q[:], b1[:], ALU.mult)
+        nc.vector.tensor_tensor(qc[:], q[:], c1[:], ALU.mult)
+        nc.vector.scalar_tensor_tensor(e2[:], pa[:], 2.0, qb[:], ALU.mult, ALU.add)
+        nc.vector.scalar_tensor_tensor(e3[:], qc[:], 2.0, pb[:], ALU.mult, ALU.add)
+        direct = f32("direct", J)
+        nc.vector.scalar_tensor_tensor(direct[:], gq[:], 0.25, sq[:], ALU.subtract, ALU.mult)
+        nc.vector.tensor_tensor(second2[:].indirect(list2[:]), e2[:], k3[:], ALU.mult)
+        nc.vector.tensor_tensor(second3[:].indirect(list3[:]), e3[:], k3[:], ALU.mult)
+
+        part = f32("part", J)
+        nc.vector.tensor_tensor(part[:], second2[:], direct[:], ALU.subtract)
+        total = f32("total", J)
+        ha = f32("ha", J)
+        y = f32("y", J)
+        for h in range(2):
+            nc.vector.tensor_tensor(total[:, halves[h]], part[:, halves[h]], second3[:, halves[h]], ALU.add)
+        for h in range(2):
+            nc.vector.tensor_tensor(ha[:, halves[h]], total[:, halves[h]], sig[:, halves[h]], ALU.mult)
+        for h in range(2):
+            nc.vector.scalar_tensor_tensor(
+                y[:, halves[h]], ha[:, halves[h]], gain[:], base_sb[:, halves[h]], ALU.mult, ALU.add
+            )
+            nc.sync.dma_start(out[:, halves[h]], y[:, halves[h]])

@@ -37,24 +37,26 @@ def tile_attend_gppairshare_kernel(tc, tab_words, tab_scales, w1, bias, reserve,
             return sb.tile([P, width], F32, name=name, align_bytes=64)
 
         table_scales = sb.tile([P, T], U8, name="table_scales", align_bytes=64)
-        nc.gpsimd.memset(table_scales[:].bitcast(I32), 0)
+        nc.vector.memset(table_scales[:].bitcast(I32), 0)
         first2, first3, second2, second3 = (f32(n, J) for n in ("first2", "first3", "second2", "second3"))
         for window in (first2, first3, second2, second3):
             nc.vector.memset(window[:], 0.0)
 
         slots = lists.tile([P, J // LIST_ROWS], U16, name="slots")
         nc.sync.dma_start(slots[:], offs)
+        bias_col = f32("bias_col", 1)
+        nc.sync.dma_start(bias_col[:], bias)
         w1_raw = sb.tile([P, PACK, R], F32, name="w1_raw")
         nc.sync.dma_start(w1_raw[:], w1.rearrange("(p t) n -> p t n", t=PACK))
-        table_words = sb.tile([P, T], U16, name="table_words", align_bytes=64)
-        nc.sync.dma_start(table_words[:].bitcast(I32), tab_words[0].bitcast(I32))
         for quad in range(4):
-            nc.scalar.dma_start(
+            nc.sync.dma_start(
                 table_scales[32 * quad : 32 * quad + 4, :].bitcast(I32),
                 tab_scales[0, 4 * quad : 4 * quad + 4, :].bitcast(I32),
             )
-        bias_col = f32("bias_col", 1)
-        nc.sync.dma_start(bias_col[:], bias)
+        table_words = sb.tile([P, T], U16, name="table_words", align_bytes=64)
+        nc.sync.dma_start(table_words[:].bitcast(I32), tab_words[0].bitcast(I32))
+        rho = f32("rho", 1)
+        nc.sync.dma_start(rho[:], reserve)
         dy_raw = sb.tile([P, PACK, M], F32, name="dy_raw")
         nc.sync.dma_start(dy_raw[:], dy.rearrange("(p t) n -> p t n", t=PACK))
         wo_raw = sb.tile([P, PACK, R], F32, name="wo_raw")
@@ -63,15 +65,13 @@ def tile_attend_gppairshare_kernel(tc, tab_words, tab_scales, w1, bias, reserve,
         nc.sync.dma_start(list2[:], offs2)
         list3 = lists.tile([P, M // LIST_ROWS], U16, name="list3")
         nc.sync.dma_start(list3[:], offs3)
-        rho = f32("rho", 1)
-        nc.sync.dma_start(rho[:], reserve)
         gain = f32("gain", 1)
         nc.sync.dma_start(gain[:], og)
         base_sb = f32("base_sb", J)
         nc.sync.dma_start(base_sb[:], base)
 
         neg_bias = f32("neg_bias", 1)
-        nc.gpsimd.tensor_scalar(neg_bias[:], bias_col[:], -1.0, 0.0, ALU.mult, ALU.add)
+        nc.vector.tensor_scalar(neg_bias[:], bias_col[:], -1.0, None, ALU.mult)
 
         def interleave(copy, raw, width, name):
             grouped = sb.tile([P, width, PACK], BF16, name=name + "_bf16", align_bytes=64)
@@ -108,6 +108,8 @@ def tile_attend_gppairshare_kernel(tc, tab_words, tab_scales, w1, bias, reserve,
             )
             nc.scalar.activation(nsig[:, halves[h]], a[:], ACT.Sigmoid, bias=neg_bias[:], scale=-1.0)
             sums.append(a)
+        neg_rho = f32("neg_rho", 1)
+        nc.vector.tensor_scalar(neg_rho[:], rho[:], -1.0, None, ALU.mult)
         for h in range(2):
             nc.vector.tensor_scalar(z[:, halves[h]], sums[h][:], bias_col[:], None, ALU.add)
 
@@ -133,7 +135,7 @@ def tile_attend_gppairshare_kernel(tc, tab_words, tab_scales, w1, bias, reserve,
         t = f32("t", M)
         nc.vector.scalar_tensor_tensor(t[:], v[:], 1.0, u[:], ALU.add, ALU.mult)
         root = f32("root", M)
-        nc.scalar.activation(root[:], t[:], ACT.Abs_reciprocal_sqrt, bias=rho[:])
+        nc.scalar.activation(root[:], t[:], ACT.Abs_reciprocal_sqrt, bias=neg_rho[:], scale=-1.0)
         sig = f32("sig", J)
         r_abs = sig[:, 0:M]
         nc.scalar.activation(r_abs, root[:], ACT.Square)
@@ -142,23 +144,35 @@ def tile_attend_gppairshare_kernel(tc, tab_words, tab_scales, w1, bias, reserve,
 
         vr = f32("vr", M)
         nc.vector.tensor_scalar(vr[:], v[:], rho[:], None, ALU.mult)
+        vm = f32("vm", M)
+        nc.vector.tensor_scalar(vm[:], v[:], -2.0, -2.0, ALU.mult, ALU.add)
         uw = f32("uw", M)
         nc.vector.scalar_tensor_tensor(uw[:], u[:], rho[:], u[:], ALU.add, ALU.mult)
         y1 = f32("y1", M)
         nc.vector.scalar_tensor_tensor(y1[:], v[:], 1.0, u[:], ALU.subtract, ALU.mult)
         a1 = f32("a1", M)
-        nc.vector.scalar_tensor_tensor(a1[:], v[:], 1.0, vr[:], ALU.add, ALU.mult)
+        nc.vector.tensor_tensor(a1[:], vm[:], vr[:], ALU.mult)
         c1 = f32("c1", M)
-        nc.vector.tensor_tensor(c1[:], uw[:], u[:], ALU.mult)
+        nc.vector.scalar_tensor_tensor(c1[:], uw[:], -2.0, u[:], ALU.mult, ALU.mult)
         b1 = f32("b1", M)
-        nc.vector.tensor_scalar(b1[:], y1[:], rho[:], rho[:], ALU.subtract, ALU.mult)
+        nc.vector.tensor_scalar(b1[:], y1[:], rho[:], neg_rho[:], ALU.subtract, ALU.mult)
 
         k2 = f32("k2", M)
         nc.vector.tensor_tensor(k2[:], r2[:], c0[:], ALU.mult)
         r_signed = f32("r_signed", M)
         nc.vector.scalar_tensor_tensor(r_signed[:], t[:], rho[:], r2[:], ALU.add, ALU.mult)
-        nc.vector.tensor_tensor(first2[:].indirect(list2[:]), vr[:], k2[:], ALU.mult)
-        nc.vector.tensor_tensor(first3[:].indirect(list3[:]), uw[:], k2[:], ALU.mult)
+        g2 = f32("g2", M)
+        nc.vector.tensor_tensor(g2[:], vr[:], k2[:], ALU.mult)
+        nc.vector.tensor_copy(first2[:].indirect(list2[:]), g2[:])
+        g3 = vr
+        nc.gpsimd.tensor_tensor(g3[:], uw[:], k2[:], ALU.mult)
+        nc.vector.tensor_copy(first3[:].indirect(list3[:]), g3[:])
+        k3 = k2
+        nc.gpsimd.tensor_tensor(k3[:], r_signed[:], k2[:], ALU.mult)
+        huu, huv, hvv = (f32(n, M) for n in ("huu", "huv", "hvv"))
+        nc.gpsimd.tensor_tensor(huu[:], a1[:], k3[:], ALU.mult)
+        nc.gpsimd.tensor_tensor(huv[:], b1[:], k3[:], ALU.mult)
+        nc.gpsimd.tensor_tensor(hvv[:], c1[:], k3[:], ALU.mult)
 
         nc.scalar.activation(sig[:], nsig[:], ACT.Identity, bias=1.0, scale=-1.0)
         sig2 = f32("sig2", J)
@@ -174,8 +188,6 @@ def tile_attend_gppairshare_kernel(tc, tab_words, tab_scales, w1, bias, reserve,
             nc.vector.scalar_tensor_tensor(
                 hdh1[:, halves[h]], dh1[:, halves[h]], 2.0, sig2[:, halves[h]], ALU.mult, ALU.mult
             )
-        k3 = f32("k3", M)
-        nc.vector.scalar_tensor_tensor(k3[:], r_signed[:], -1.0, k2[:], ALU.mult, ALU.mult)
         sq = f32("sq", J)
         nc.scalar.activation(sq[:], dh1[:], ACT.Square, scale=math.sqrt(2.0))
 
@@ -183,20 +195,26 @@ def tile_attend_gppairshare_kernel(tc, tab_words, tab_scales, w1, bias, reserve,
         q = f32("q", M)
         nc.vector.tensor_copy(p[:], hdh1[:].indirect(list2[:]))
         nc.vector.tensor_copy(q[:], hdh1[:].indirect(list3[:]))
-        pa, qb, pb, qc, e2, e3 = (f32(n, M) for n in ("pa", "qb", "pb", "qc", "e2", "e3"))
-        nc.vector.tensor_tensor(pa[:], p[:], a1[:], ALU.mult)
-        nc.vector.tensor_tensor(pb[:], p[:], b1[:], ALU.mult)
-        nc.vector.tensor_tensor(qb[:], q[:], b1[:], ALU.mult)
-        nc.vector.tensor_tensor(qc[:], q[:], c1[:], ALU.mult)
-        nc.vector.scalar_tensor_tensor(e2[:], pa[:], 2.0, qb[:], ALU.mult, ALU.add)
-        nc.vector.scalar_tensor_tensor(e3[:], qc[:], 2.0, pb[:], ALU.mult, ALU.add)
+        pa, qb, e2, e3 = (f32(n, M) for n in ("pa", "qb", "e2", "e3"))
         direct = f32("direct", J)
-        nc.vector.scalar_tensor_tensor(direct[:], gq[:], 0.25, sq[:], ALU.subtract, ALU.mult)
-        nc.vector.tensor_tensor(second2[:].indirect(list2[:]), e2[:], k3[:], ALU.mult)
-        nc.vector.tensor_tensor(second3[:].indirect(list3[:]), e3[:], k3[:], ALU.mult)
+        nc.vector.tensor_tensor(pa[:], p[:], huu[:], ALU.mult)
+        nc.vector.tensor_tensor(qb[:], q[:], huv[:], ALU.mult)
+        nc.vector.scalar_tensor_tensor(
+            direct[:, halves[0]], gq[:, halves[0]], 0.25, sq[:, halves[0]], ALU.subtract, ALU.mult
+        )
+        nc.vector.tensor_tensor(e2[:], pa[:], qb[:], ALU.add)
+        nc.vector.scalar_tensor_tensor(
+            direct[:, halves[1]], gq[:, halves[1]], 0.25, sq[:, halves[1]], ALU.subtract, ALU.mult
+        )
+        nc.vector.tensor_copy(second2[:].indirect(list2[:]), e2[:])
+        pb, qc = pa, qb
+        nc.gpsimd.tensor_tensor(pb[:], p[:], huv[:], ALU.mult)
+        nc.gpsimd.tensor_tensor(qc[:], q[:], hvv[:], ALU.mult)
+        nc.gpsimd.tensor_tensor(e3[:], pb[:], qc[:], ALU.add)
+        nc.vector.tensor_copy(second3[:].indirect(list3[:]), e3[:])
 
         part = f32("part", J)
-        nc.vector.tensor_tensor(part[:], second2[:], direct[:], ALU.subtract)
+        nc.gpsimd.tensor_tensor(part[:], second2[:], direct[:], ALU.subtract)
         total = f32("total", J)
         ha = f32("ha", J)
         y = f32("y", J)

@@ -53,14 +53,14 @@ def tile_attend_gppairshare_kernel(tc, tab_words, tab_scales, w1, bias, reserve,
                 table_scales[32 * quad : 32 * quad + 4, :].bitcast(I32),
                 tab_scales[0, 4 * quad : 4 * quad + 4, :].bitcast(I32),
             )
-        table_words = sb.tile([P, T], U16, name="table_words", align_bytes=64)
+        table_words = sb.tile([P, T], U16, name="table_words", tag="table_words", align_bytes=64)
         nc.sync.dma_start(table_words[:].bitcast(I32), tab_words[0].bitcast(I32))
-        rho = f32("rho", 1)
-        nc.sync.dma_start(rho[:], reserve)
         dy_raw = sb.tile([P, PACK, M], F32, name="dy_raw")
         nc.sync.dma_start(dy_raw[:], dy.rearrange("(p t) n -> p t n", t=PACK))
         wo_raw = sb.tile([P, PACK, R], F32, name="wo_raw")
         nc.sync.dma_start(wo_raw[:], wo.rearrange("(p t) n -> p t n", t=PACK))
+        rho = f32("rho", 1)
+        nc.sync.dma_start(rho[:], reserve)
         list2 = lists.tile([P, M // LIST_ROWS], U16, name="list2")
         nc.sync.dma_start(list2[:], offs2)
         list3 = lists.tile([P, M // LIST_ROWS], U16, name="list3")
@@ -73,18 +73,21 @@ def tile_attend_gppairshare_kernel(tc, tab_words, tab_scales, w1, bias, reserve,
         neg_bias = f32("neg_bias", 1)
         nc.vector.tensor_scalar(neg_bias[:], bias_col[:], -1.0, None, ALU.mult)
 
-        def interleave(copy, raw, width, name):
-            grouped = sb.tile([P, width, PACK], BF16, name=name + "_bf16", align_bytes=64)
-            copy(grouped[:], raw[:].rearrange("p t n -> p n t"))
-            return grouped
-
         def quantize(grouped, width, name):
             codes = sb.tile([P, width], U32, name=name + "_codes", align_bytes=64)
             scales = sb.tile([P, width], U8, name=name + "_scales", align_bytes=64)
-            nc.vector.quantize_mx(codes[:].bitcast(FP8X4), scales[:], grouped[:].rearrange("p n t -> p (n t)"))
+            nc.vector.quantize_mx(codes[:].bitcast(FP8X4), scales[:], grouped)
             return codes, scales
 
-        w1_codes, w1_scales = quantize(interleave(nc.vector.tensor_copy, w1_raw, R, "w1"), R, "w1")
+        def words_of(flat):
+            return flat.rearrange("p (n t) -> p n t", t=PACK)
+
+        def by_column(raw):
+            return raw[:].rearrange("p t n -> p n t")
+
+        w1_bf16 = sb.tile([P, PACK * R], BF16, name="w1_bf16", align_bytes=64)
+        nc.vector.tensor_copy(words_of(w1_bf16[:]), by_column(w1_raw))
+        w1_codes, w1_scales = quantize(w1_bf16[:], R, "w1")
         picked_scales = sb.tile([P, J], U8, name="picked_scales", align_bytes=64)
         nc.vector.tensor_copy(picked_scales[:], table_scales[:].indirect(slots[:]))
 
@@ -108,13 +111,19 @@ def tile_attend_gppairshare_kernel(tc, tab_words, tab_scales, w1, bias, reserve,
             )
             nc.scalar.activation(nsig[:, halves[h]], a[:], ACT.Sigmoid, bias=neg_bias[:], scale=-1.0)
             sums.append(a)
-        neg_rho = f32("neg_rho", 1)
-        nc.vector.tensor_scalar(neg_rho[:], rho[:], -1.0, None, ALU.mult)
+        late = sb.tile([P, T // 2], F32, name="late", tag="table_words", align_bytes=64)
+        dy_bf16 = late[:, 0 : 2 * M].bitcast(BF16)
+        wo_bf16 = late[:, 2 * M : 2 * (M + R)].bitcast(BF16)
+        neg_rho, rho2 = (late[:, 2 * (M + R) + i : 2 * (M + R) + i + 1] for i in range(2))
         for h in range(2):
             nc.vector.tensor_scalar(z[:, halves[h]], sums[h][:], bias_col[:], None, ALU.add)
 
-        dy_codes, dy_scales = quantize(interleave(nc.vector.tensor_copy, dy_raw, M, "dy"), M, "dy")
-        wo_codes, wo_scales = quantize(interleave(nc.vector.tensor_copy, wo_raw, R, "wo"), R, "wo")
+        nc.vector.tensor_copy(words_of(dy_bf16), by_column(dy_raw))
+        nc.vector.tensor_copy(words_of(wo_bf16), by_column(wo_raw))
+        dy_codes, dy_scales = quantize(dy_bf16, M, "dy")
+        wo_codes, wo_scales = quantize(wo_bf16, R, "wo")
+        nc.vector.tensor_scalar(neg_rho, rho[:], -1.0, None, ALU.mult)
+        nc.vector.tensor_scalar(rho2, rho[:], rho[:], None, ALU.mult)
         c0 = ps.tile([P, M], F32, name="c0")
         nc.tensor.matmul_mx(
             c0[:], wo_codes[:].bitcast(FP8X4), wo_scales[:], dy_codes[:].bitcast(FP8X4), dy_scales[:],
@@ -130,42 +139,44 @@ def tile_attend_gppairshare_kernel(tc, tab_words, tab_scales, w1, bias, reserve,
 
         u = f32("u", M)
         v = f32("v", M)
-        nc.vector.tensor_copy(u[:], h1[:].indirect(list2[:]))
         nc.vector.tensor_copy(v[:], h1[:].indirect(list3[:]))
+        nc.vector.tensor_copy(u[:], h1[:].indirect(list2[:]))
         t = f32("t", M)
         nc.vector.scalar_tensor_tensor(t[:], v[:], 1.0, u[:], ALU.add, ALU.mult)
+        pair_halves = [slice(h * M // 2, (h + 1) * M // 2) for h in range(2)]
         root = f32("root", M)
-        nc.scalar.activation(root[:], t[:], ACT.Abs_reciprocal_sqrt, bias=neg_rho[:], scale=-1.0)
+        r_abs = f32("r_abs", M)
         sig = f32("sig", J)
-        r_abs = sig[:, 0:M]
-        nc.scalar.activation(r_abs, root[:], ACT.Square)
-        r2 = f32("r2", M)
-        nc.scalar.activation(r2[:], r_abs, ACT.Square)
+        r2 = sig[:, 0:M]
+        for cols in pair_halves:
+            nc.scalar.activation(root[:, cols], t[:, cols], ACT.Abs_reciprocal_sqrt, bias=neg_rho, scale=-1.0)
+        for cols in pair_halves:
+            nc.scalar.activation(r_abs[:, cols], root[:, cols], ACT.Square)
+        for cols in pair_halves:
+            nc.scalar.activation(sig[:, cols], r_abs[:, cols], ACT.Square)
 
         vr = f32("vr", M)
         nc.vector.tensor_scalar(vr[:], v[:], rho[:], None, ALU.mult)
-        vm = f32("vm", M)
-        nc.vector.tensor_scalar(vm[:], v[:], -2.0, -2.0, ALU.mult, ALU.add)
         uw = f32("uw", M)
         nc.vector.scalar_tensor_tensor(uw[:], u[:], rho[:], u[:], ALU.add, ALU.mult)
         y1 = f32("y1", M)
         nc.vector.scalar_tensor_tensor(y1[:], v[:], 1.0, u[:], ALU.subtract, ALU.mult)
         a1 = f32("a1", M)
-        nc.vector.tensor_tensor(a1[:], vm[:], vr[:], ALU.mult)
+        nc.vector.scalar_tensor_tensor(a1[:], v[:], 1.0, vr[:], ALU.add, ALU.mult)
         c1 = f32("c1", M)
-        nc.vector.scalar_tensor_tensor(c1[:], uw[:], -2.0, u[:], ALU.mult, ALU.mult)
-        b1 = f32("b1", M)
-        nc.vector.tensor_scalar(b1[:], y1[:], rho[:], neg_rho[:], ALU.subtract, ALU.mult)
+        nc.vector.tensor_tensor(c1[:], uw[:], u[:], ALU.mult)
+        b1 = r_abs
+        nc.scalar.activation(b1[:], y1[:], ACT.Identity, bias=rho2, scale=neg_rho)
 
         k2 = f32("k2", M)
-        nc.vector.tensor_tensor(k2[:], r2[:], c0[:], ALU.mult)
+        nc.vector.tensor_tensor(k2[:], r2, c0[:], ALU.mult)
         r_signed = f32("r_signed", M)
-        nc.vector.scalar_tensor_tensor(r_signed[:], t[:], rho[:], r2[:], ALU.add, ALU.mult)
+        nc.vector.scalar_tensor_tensor(r_signed[:], t[:], rho[:], r2, ALU.add, ALU.mult)
         g2 = f32("g2", M)
         nc.vector.tensor_tensor(g2[:], vr[:], k2[:], ALU.mult)
+        g3 = f32("g3", M)
+        nc.vector.tensor_tensor(g3[:], uw[:], k2[:], ALU.mult)
         nc.vector.tensor_copy(first2[:].indirect(list2[:]), g2[:])
-        g3 = vr
-        nc.gpsimd.tensor_tensor(g3[:], uw[:], k2[:], ALU.mult)
         nc.vector.tensor_copy(first3[:].indirect(list3[:]), g3[:])
         k3 = k2
         nc.gpsimd.tensor_tensor(k3[:], r_signed[:], k2[:], ALU.mult)
@@ -179,6 +190,8 @@ def tile_attend_gppairshare_kernel(tc, tab_words, tab_scales, w1, bias, reserve,
         nc.scalar.activation(sig2[:], sig[:], ACT.Square)
         gq = f32("gq", J)
         nc.scalar.activation(gq[:], sig[:], ACT.Square, bias=-0.5)
+        slope = f32("slope", J)
+        nc.scalar.activation(slope[:], gq[:], ACT.Identity, bias=0.25, scale=-1.0)
 
         dh1 = f32("dh1", J)
         hdh1 = f32("hdh1", J)
@@ -195,26 +208,22 @@ def tile_attend_gppairshare_kernel(tc, tab_words, tab_scales, w1, bias, reserve,
         q = f32("q", M)
         nc.vector.tensor_copy(p[:], hdh1[:].indirect(list2[:]))
         nc.vector.tensor_copy(q[:], hdh1[:].indirect(list3[:]))
+        mixed = f32("mixed", J)
+        pb, qc = mixed[:, halves[0]], mixed[:, halves[1]]
         pa, qb, e2, e3 = (f32(n, M) for n in ("pa", "qb", "e2", "e3"))
-        direct = f32("direct", J)
-        nc.vector.tensor_tensor(pa[:], p[:], huu[:], ALU.mult)
+        nc.vector.scalar_tensor_tensor(pa[:], p[:], -2.0, huu[:], ALU.mult, ALU.mult)
+        nc.vector.tensor_tensor(pb, p[:], huv[:], ALU.mult)
         nc.vector.tensor_tensor(qb[:], q[:], huv[:], ALU.mult)
-        nc.vector.scalar_tensor_tensor(
-            direct[:, halves[0]], gq[:, halves[0]], 0.25, sq[:, halves[0]], ALU.subtract, ALU.mult
-        )
+        nc.vector.scalar_tensor_tensor(qc, q[:], -2.0, hvv[:], ALU.mult, ALU.mult)
         nc.vector.tensor_tensor(e2[:], pa[:], qb[:], ALU.add)
-        nc.vector.scalar_tensor_tensor(
-            direct[:, halves[1]], gq[:, halves[1]], 0.25, sq[:, halves[1]], ALU.subtract, ALU.mult
-        )
+        nc.vector.tensor_tensor(e3[:], pb, qc, ALU.add)
         nc.vector.tensor_copy(second2[:].indirect(list2[:]), e2[:])
-        pb, qc = pa, qb
-        nc.gpsimd.tensor_tensor(pb[:], p[:], huv[:], ALU.mult)
-        nc.gpsimd.tensor_tensor(qc[:], q[:], hvv[:], ALU.mult)
-        nc.gpsimd.tensor_tensor(e3[:], pb[:], qc[:], ALU.add)
         nc.vector.tensor_copy(second3[:].indirect(list3[:]), e3[:])
-
+        direct = mixed
+        nc.gpsimd.tensor_tensor(direct[:], slope[:], sq[:], ALU.mult)
         part = f32("part", J)
-        nc.gpsimd.tensor_tensor(part[:], second2[:], direct[:], ALU.subtract)
+        for cols in halves:
+            nc.gpsimd.tensor_tensor(part[:, cols], second2[:, cols], direct[:, cols], ALU.add)
         total = f32("total", J)
         ha = f32("ha", J)
         y = f32("y", J)

@@ -42,12 +42,12 @@ def tile_attend_gppairshare_kernel(tc, tab_words, tab_scales, w1, bias, reserve,
         for window in (first2, first3, second2, second3):
             nc.vector.memset(window[:], 0.0)
 
+        w1_raw = sb.tile([P, PACK, R], F32, name="w1_raw")
+        nc.sync.dma_start(w1_raw[:], w1.rearrange("(p t) n -> p t n", t=PACK))
         slots = lists.tile([P, J // LIST_ROWS], U16, name="slots")
         nc.sync.dma_start(slots[:], offs)
         bias_col = f32("bias_col", 1)
         nc.sync.dma_start(bias_col[:], bias)
-        w1_raw = sb.tile([P, PACK, R], F32, name="w1_raw")
-        nc.sync.dma_start(w1_raw[:], w1.rearrange("(p t) n -> p t n", t=PACK))
         for quad in range(4):
             nc.sync.dma_start(
                 table_scales[32 * quad : 32 * quad + 4, :].bitcast(I32),
@@ -70,8 +70,6 @@ def tile_attend_gppairshare_kernel(tc, tab_words, tab_scales, w1, bias, reserve,
         base_sb = f32("base_sb", J)
         nc.sync.dma_start(base_sb[:], base)
 
-        neg_bias = f32("neg_bias", 1)
-        nc.vector.tensor_scalar(neg_bias[:], bias_col[:], -1.0, None, ALU.mult)
 
         def quantize(grouped, width, name):
             codes = sb.tile([P, width], U32, name=name + "_codes", align_bytes=64)
@@ -87,6 +85,8 @@ def tile_attend_gppairshare_kernel(tc, tab_words, tab_scales, w1, bias, reserve,
 
         w1_bf16 = sb.tile([P, PACK * R], BF16, name="w1_bf16", align_bytes=64)
         nc.vector.tensor_copy(words_of(w1_bf16[:]), by_column(w1_raw))
+        neg_bias = f32("neg_bias", 1)
+        nc.vector.tensor_scalar(neg_bias[:], bias_col[:], -1.0, None, ALU.mult)
         w1_codes, w1_scales = quantize(w1_bf16[:], R, "w1")
         picked_scales = sb.tile([P, J], U8, name="picked_scales", align_bytes=64)
         nc.vector.tensor_copy(picked_scales[:], table_scales[:].indirect(slots[:]))
@@ -202,33 +202,35 @@ def tile_attend_gppairshare_kernel(tc, tab_words, tab_scales, w1, bias, reserve,
                 hdh1[:, halves[h]], dh1[:, halves[h]], 2.0, sig2[:, halves[h]], ALU.mult, ALU.mult
             )
         sq = f32("sq", J)
-        nc.scalar.activation(sq[:], dh1[:], ACT.Square, scale=math.sqrt(2.0))
+        for cols in halves:
+            nc.scalar.activation(sq[:, cols], dh1[:, cols], ACT.Square, scale=math.sqrt(2.0))
+        direct0 = sig2[:, halves[1]]
+        nc.gpsimd.tensor_tensor(direct0, slope[:, halves[0]], sq[:, halves[0]], ALU.mult)
 
         p = f32("p", M)
         q = f32("q", M)
         nc.vector.tensor_copy(p[:], hdh1[:].indirect(list2[:]))
         nc.vector.tensor_copy(q[:], hdh1[:].indirect(list3[:]))
-        mixed = f32("mixed", J)
-        pb, qc = mixed[:, halves[0]], mixed[:, halves[1]]
         pa, qb, e2, e3 = (f32(n, M) for n in ("pa", "qb", "e2", "e3"))
+        pb, qc = huu, q
         nc.vector.scalar_tensor_tensor(pa[:], p[:], -2.0, huu[:], ALU.mult, ALU.mult)
-        nc.vector.tensor_tensor(pb, p[:], huv[:], ALU.mult)
         nc.vector.tensor_tensor(qb[:], q[:], huv[:], ALU.mult)
-        nc.vector.scalar_tensor_tensor(qc, q[:], -2.0, hvv[:], ALU.mult, ALU.mult)
+        nc.vector.tensor_tensor(pb[:], p[:], huv[:], ALU.mult)
         nc.vector.tensor_tensor(e2[:], pa[:], qb[:], ALU.add)
-        nc.vector.tensor_tensor(e3[:], pb, qc, ALU.add)
+        nc.vector.scalar_tensor_tensor(qc[:], q[:], -2.0, hvv[:], ALU.mult, ALU.mult)
         nc.vector.tensor_copy(second2[:].indirect(list2[:]), e2[:])
+        nc.gpsimd.tensor_tensor(e3[:], pb[:], qc[:], ALU.add)
         nc.vector.tensor_copy(second3[:].indirect(list3[:]), e3[:])
-        direct = mixed
-        nc.gpsimd.tensor_tensor(direct[:], slope[:], sq[:], ALU.mult)
-        part = f32("part", J)
-        for cols in halves:
-            nc.gpsimd.tensor_tensor(part[:, cols], second2[:, cols], direct[:, cols], ALU.add)
+        direct1 = pb
+        nc.gpsimd.tensor_tensor(direct1[:], slope[:, halves[1]], sq[:, halves[1]], ALU.mult)
+        parts = (sq[:, halves[1]], slope[:, halves[1]])
+        for cols, part, direct in zip(halves, parts, (direct0, direct1[:])):
+            nc.gpsimd.tensor_tensor(part, second2[:, cols], direct, ALU.add)
         total = f32("total", J)
         ha = f32("ha", J)
         y = f32("y", J)
         for h in range(2):
-            nc.vector.tensor_tensor(total[:, halves[h]], part[:, halves[h]], second3[:, halves[h]], ALU.add)
+            nc.vector.tensor_tensor(total[:, halves[h]], parts[h], second3[:, halves[h]], ALU.add)
         for h in range(2):
             nc.vector.tensor_tensor(ha[:, halves[h]], total[:, halves[h]], sig[:, halves[h]], ALU.mult)
         for h in range(2):

import math
from contextlib import ExitStack

import concourse.mybir as mybir

K, R, F, T, J, M = 512, 128, 512, 2048, 512, 256
FLOPS = 2 * K * R * J + 2 * F * R * M

F32 = mybir.dt.float32
BF16 = mybir.dt.bfloat16
I32 = mybir.dt.int32
U32 = mybir.dt.uint32
U16 = mybir.dt.uint16
U8 = mybir.dt.uint8
FP8X4 = mybir.dt.float8_e4m3fn_x4
FP4X4 = mybir.dt.float4_e2m1fn_x4
ACT = mybir.ActivationFunctionType
ALU = mybir.AluOpType

P = 128
PACK = 4
HALF = J // 2
LIST_ROWS = 16
TINY = 2.0 ** -60


def tile_attend_gppairshare_kernel(tc, tab_words, tab_scales, w1, bias, reserve, wo, dy, og, base, offs, offs2, offs3, out):
    nc = tc.nc
    halves = [slice(h * HALF, (h + 1) * HALF) for h in range(2)]

    with ExitStack() as ctx:
        lists = ctx.enter_context(tc.tile_pool(name="lists", bufs=1))
        sb = ctx.enter_context(tc.tile_pool(name="sb", bufs=1))
        ps = ctx.enter_context(tc.psum_pool(name="ps", bufs=1))

        def f32(name, width):
            return sb.tile([P, width], F32, name=name, align_bytes=64)

        table_scales = sb.tile([P, T], U8, name="table_scales", align_bytes=64)
        nc.vector.memset(table_scales[:].bitcast(I32), 0)
        first2, first3, second2, second3 = (f32(n, J) for n in ("first2", "first3", "second2", "second3"))
        for window in (first2, first3, second2, second3):
            nc.vector.memset(window[:], 0.0)

        w1_raw = sb.tile([P, PACK, R], F32, name="w1_raw")
        nc.sync.dma_start(w1_raw[:], w1.rearrange("(p t) n -> p t n", t=PACK))
        slots = lists.tile([P, J // LIST_ROWS], U16, name="slots")
        nc.sync.dma_start(slots[:], offs)
        bias_col = f32("bias_col", 1)
        nc.sync.dma_start(bias_col[:], bias)
        for quad in range(4):
            nc.sync.dma_start(
                table_scales[32 * quad : 32 * quad + 4, :].bitcast(I32),
                tab_scales[0, 4 * quad : 4 * quad + 4, :].bitcast(I32),
            )
        table_words = sb.tile([P, T], U16, name="table_words", tag="table_words", align_bytes=64)
        nc.sync.dma_start(table_words[:].bitcast(I32), tab_words[0].bitcast(I32))
        dy_raw = sb.tile([P, PACK, M], F32, name="dy_raw")
        nc.sync.dma_start(dy_raw[:], dy.rearrange("(p t) n -> p t n", t=PACK))
        wo_raw = sb.tile([P, PACK, R], F32, name="wo_raw")
        nc.sync.dma_start(wo_raw[:], wo.rearrange("(p t) n -> p t n", t=PACK))
        rho = f32("rho", 1)
        nc.sync.dma_start(rho[:], reserve)
        list2 = lists.tile([P, M // LIST_ROWS], U16, name="list2")
        nc.sync.dma_start(list2[:], offs2)
        list3 = lists.tile([P, M // LIST_ROWS], U16, name="list3")
        nc.sync.dma_start(list3[:], offs3)
        gain = f32("gain", 1)
        nc.sync.dma_start(gain[:], og)
        base_sb = f32("base_sb", J)
        nc.sync.dma_start(base_sb[:], base)


        def quantize(grouped, width, name):
            codes = sb.tile([P, width], U32, name=name + "_codes", align_bytes=64)
            scales = sb.tile([P, width], U8, name=name + "_scales", align_bytes=64)
            nc.vector.quantize_mx(codes[:].bitcast(FP8X4), scales[:], grouped)
            return codes, scales

        def words_of(flat):
            return flat.rearrange("p (n t) -> p n t", t=PACK)

        def by_column(raw):
            return raw[:].rearrange("p t n -> p n t")

        w1_bf16 = sb.tile([P, PACK * R], BF16, name="w1_bf16", align_bytes=64)
        nc.vector.tensor_copy(words_of(w1_bf16[:]), by_column(w1_raw))
        neg_bias = f32("neg_bias", 1)
        nc.vector.tensor_scalar(neg_bias[:], bias_col[:], -1.0, None, ALU.mult)
        w1_codes, w1_scales = quantize(w1_bf16[:], R, "w1")
        picked_scales = sb.tile([P, J], U8, name="picked_scales", align_bytes=64)
        nc.vector.tensor_copy(picked_scales[:], table_scales[:].indirect(slots[:]))

        picked = []
        for h in range(2):
            cols = slice(h * HALF // LIST_ROWS, (h + 1) * HALF // LIST_ROWS)
            words = sb.tile([P, HALF], U16, name="picked_words%d" % h, align_bytes=64)
            nc.vector.tensor_copy(words[:], table_words[:].indirect(slots[:, cols]))
            picked.append(words)

        z = f32("z", J)
        nsig = f32("nsig", J)
        log_nsig = f32("log_nsig", J)
        h1 = f32("h1", J)
        sums = []
        for h in range(2):
            a = ps.tile([P, HALF], F32, name="a%d" % h)
            nc.tensor.matmul_mx(
                a[:], w1_codes[:].bitcast(FP8X4), w1_scales[:],
                picked[h][:].bitcast(FP4X4), picked_scales[:, halves[h]], start=True, stop=True,
            )
            nc.scalar.activation(nsig[:, halves[h]], a[:], ACT.Sigmoid, bias=neg_bias[:], scale=-1.0)
            sums.append(a)
        late = sb.tile([P, T // 2], F32, name="late", tag="table_words", align_bytes=64)
        dy_bf16 = late[:, 0 : 2 * M].bitcast(BF16)
        wo_bf16 = late[:, 2 * M : 2 * (M + R)].bitcast(BF16)
        neg_rho, rho2 = (late[:, 2 * (M + R) + i : 2 * (M + R) + i + 1] for i in range(2))
        for h in range(2):
            nc.vector.tensor_scalar(z[:, halves[h]], sums[h][:], bias_col[:], None, ALU.add)

        nc.vector.tensor_copy(words_of(dy_bf16), by_column(dy_raw))
        nc.vector.tensor_copy(words_of(wo_bf16), by_column(wo_raw))
        dy_codes, dy_scales = quantize(dy_bf16, M, "dy")
        wo_codes, wo_scales = quantize(wo_bf16, R, "wo")
        nc.vector.tensor_scalar(neg_rho, rho[:], -1.0, None, ALU.mult)
        nc.vector.tensor_scalar(rho2, rho[:], rho[:], None, ALU.mult)
        c0 = ps.tile([P, M], F32, name="c0")
        nc.tensor.matmul_mx(
            c0[:], wo_codes[:].bitcast(FP8X4), wo_scales[:], dy_codes[:].bitcast(FP8X4), dy_scales[:],
            start=True, stop=True,
        )

        for h in range(2):
            nc.scalar.activation(log_nsig[:, halves[h]], nsig[:, halves[h]], ACT.Ln, bias=TINY)
        for h in range(2):
            nc.vector.scalar_tensor_tensor(
                h1[:, halves[h]], log_nsig[:, halves[h]], -1.0, z[:, halves[h]], ALU.mult, ALU.max
            )

        u = f32("u", M)
        v = f32("v", M)
        nc.vector.tensor_copy(v[:], h1[:].indirect(list3[:]))
        nc.vector.tensor_copy(u[:], h1[:].indirect(list2[:]))
        t = f32("t", M)
        nc.vector.scalar_tensor_tensor(t[:], v[:], 1.0, u[:], ALU.add, ALU.mult)
        pair_halves = [slice(h * M // 2, (h + 1) * M // 2) for h in range(2)]
        root = f32("root", M)
        r_abs = f32("r_abs", M)
        sig = f32("sig", J)
        r2 = sig[:, 0:M]
        for cols in pair_halves:
            nc.scalar.activation(root[:, cols], t[:, cols], ACT.Abs_reciprocal_sqrt, bias=neg_rho, scale=-1.0)
        for cols in pair_halves:
            nc.scalar.activation(r_abs[:, cols], root[:, cols], ACT.Square)
        for cols in pair_halves:
            nc.scalar.activation(sig[:, cols], r_abs[:, cols], ACT.Square)

        vr = f32("vr", M)
        nc.vector.tensor_scalar(vr[:], v[:], rho[:], None, ALU.mult)
        uw = f32("uw", M)
        nc.vector.scalar_tensor_tensor(uw[:], u[:], rho[:], u[:], ALU.add, ALU.mult)
        y1 = f32("y1", M)
        nc.vector.scalar_tensor_tensor(y1[:], v[:], 1.0, u[:], ALU.subtract, ALU.mult)
        a1 = f32("a1", M)
        nc.vector.scalar_tensor_tensor(a1[:], v[:], 1.0, vr[:], ALU.add, ALU.mult)
        c1 = f32("c1", M)
        nc.vector.tensor_tensor(c1[:], uw[:], u[:], ALU.mult)
        b1 = r_abs
        nc.scalar.activation(b1[:], y1[:], ACT.Identity, bias=rho2, scale=neg_rho)

        k2 = f32("k2", M)
        nc.vector.tensor_tensor(k2[:], r2, c0[:], ALU.mult)
        r_signed = f32("r_signed", M)
        nc.vector.scalar_tensor_tensor(r_signed[:], t[:], rho[:], r2, ALU.add, ALU.mult)
        g2 = f32("g2", M)
        nc.vector.tensor_tensor(g2[:], vr[:], k2[:], ALU.mult)
        g3 = f32("g3", M)
        nc.vector.tensor_tensor(g3[:], uw[:], k2[:], ALU.mult)
        nc.vector.tensor_copy(first2[:].indirect(list2[:]), g2[:])
        nc.vector.tensor_copy(first3[:].indirect(list3[:]), g3[:])
        k3 = k2
        nc.gpsimd.tensor_tensor(k3[:], r_signed[:], k2[:], ALU.mult)
        huu, huv, hvv = (f32(n, M) for n in ("huu", "huv", "hvv"))
        nc.gpsimd.tensor_tensor(huu[:], a1[:], k3[:], ALU.mult)
        nc.gpsimd.tensor_tensor(huv[:], b1[:], k3[:], ALU.mult)
        nc.gpsimd.tensor_tensor(hvv[:], c1[:], k3[:], ALU.mult)

        nc.scalar.activation(sig[:], nsig[:], ACT.Identity, bias=1.0, scale=-1.0)
        sig2 = f32("sig2", J)
        nc.scalar.activation(sig2[:], sig[:], ACT.Square)
        gq = f32("gq", J)
        nc.scalar.activation(gq[:], sig[:], ACT.Square, bias=-0.5)
        slope = f32("slope", J)
        nc.scalar.activation(slope[:], gq[:], ACT.Identity, bias=0.25, scale=-1.0)

        dh1 = f32("dh1", J)
        hdh1 = f32("hdh1", J)
        for h in range(2):
            nc.vector.tensor_tensor(dh1[:, halves[h]], first2[:, halves[h]], first3[:, halves[h]], ALU.add)
        for h in range(2):
            nc.vector.scalar_tensor_tensor(
                hdh1[:, halves[h]], dh1[:, halves[h]], 2.0, sig2[:, halves[h]], ALU.mult, ALU.mult
            )
        sq = f32("sq", J)
        for cols in halves:
            nc.scalar.activation(sq[:, cols], dh1[:, cols], ACT.Square, scale=math.sqrt(2.0))
        direct0 = sig2[:, halves[1]]
        nc.gpsimd.tensor_tensor(direct0, slope[:, halves[0]], sq[:, halves[0]], ALU.mult)

        p = f32("p", M)
        q = f32("q", M)
        nc.vector.tensor_copy(p[:], hdh1[:].indirect(list2[:]))
        nc.vector.tensor_copy(q[:], hdh1[:].indirect(list3[:]))
        pa, qb, e2, e3 = (f32(n, M) for n in ("pa", "qb", "e2", "e3"))
        pb, qc = huu, q
        nc.vector.scalar_tensor_tensor(pa[:], p[:], -2.0, huu[:], ALU.mult, ALU.mult)
        nc.vector.tensor_tensor(qb[:], q[:], huv[:], ALU.mult)
        nc.vector.tensor_tensor(pb[:], p[:], huv[:], ALU.mult)
        nc.vector.tensor_tensor(e2[:], pa[:], qb[:], ALU.add)
        nc.vector.scalar_tensor_tensor(qc[:], q[:], -2.0, hvv[:], ALU.mult, ALU.mult)
        nc.vector.tensor_copy(second2[:].indirect(list2[:]), e2[:])
        nc.gpsimd.tensor_tensor(e3[:], pb[:], qc[:], ALU.add)
        nc.vector.tensor_copy(second3[:].indirect(list3[:]), e3[:])
        direct1 = pb
        nc.gpsimd.tensor_tensor(direct1[:], slope[:, halves[1]], sq[:, halves[1]], ALU.mult)
        parts = (sq[:, halves[1]], slope[:, halves[1]])
        for cols, part, direct in zip(halves, parts, (direct0, direct1[:])):
            nc.gpsimd.tensor_tensor(part, second2[:, cols], direct, ALU.add)
        total = f32("total", J)
        ha = f32("ha", J)
        y = f32("y", J)
        for h in range(2):
            nc.vector.tensor_tensor(total[:, halves[h]], parts[h], second3[:, halves[h]], ALU.add)
        for h in range(2):
            nc.vector.tensor_tensor(ha[:, halves[h]], total[:, halves[h]], sig[:, halves[h]], ALU.mult)
        for h in range(2):
            nc.vector.scalar_tensor_tensor(
                y[:, halves[h]], ha[:, halves[h]], gain[:], base_sb[:, halves[h]], ALU.mult, ALU.add
            )
            nc.sync.dma_start(out[:, halves[h]], y[:, halves[h]])
